import numpy as np
import ml_dtypes


def mxq(x, axis, fmt="e4m3"):
    dtype, down = {"e4m3": (ml_dtypes.float8_e4m3fn, 7), "e5m2": (ml_dtypes.float8_e5m2, 14)}[fmt]
    v = np.moveaxis(np.asarray(x, np.float32).astype(ml_dtypes.bfloat16).astype(np.float64), axis, -1)
    blocks = v.reshape(v.shape[:-1] + (-1, 32))
    amax = np.abs(blocks).max(-1, keepdims=True)
    byte = np.maximum(np.where(amax > 0, np.frexp(amax)[1] - 1 + 127, 0) - down, 1)
    scale = np.exp2(byte - 127.0)
    codes = (blocks / scale).astype(np.float32).astype(dtype).astype(np.float64)
    return np.moveaxis((codes * scale).reshape(v.shape), -1, axis)


WIDE = False


def mx_kscale(k, group=512):
    if not WIDE:
        return np.ones(k)
    levels = np.array([10, -10, 5, -5, 0])
    if group != 512:
        return np.exp2(np.random.permutation(np.resize(levels, k // group))).repeat(group)
    if k % 512:
        return np.exp2(np.random.permutation(np.resize(levels, k // 32))).repeat(32)
    a = np.empty((k // 512, 16))
    for p in range(k // 512):
        a[p, :8] = np.random.permutation(np.resize(levels, 8))
        for g in range(8):
            far = levels[np.abs(levels - a[p, g]) >= 10]
            a[p, g + 8] = far[np.random.randint(len(far))]
    return np.exp2(a.ravel()).repeat(32)


def f64(x):
    return np.asarray(x).astype(np.float64)


G, D, M, N = 2, 256, 128, 512


def setup_inputs():
    n = np.random.standard_normal
    s_d = mx_kscale(D, 0)
    return {
        "x": (n((G, D, M)) / s_d[:, None] / np.sqrt(D)).astype(np.float32),
        "c": (n((G, D, N)) * s_d[:, None]).astype(np.float32),
        "gn": (np.random.uniform(0.5, 2.0, (G, 1, N))).astype(np.float32),
        "gb": (0.5 * n((G, 1, N))).astype(np.float32),
    }


def reference(x, c, gn, gb):
    xq = mxq(f64(x), 1, "e4m3")
    cq = mxq(f64(c), 1, "e4m3")
    z = xq.transpose(0, 2, 1) @ cq
    mu = np.mean(z, axis=-1, keepdims=True)
    zc = z - mu
    va = np.mean(np.square(zc), axis=-1, keepdims=True)
    y = zc / np.sqrt(va + 1e-05) * f64(gn) + f64(gb)
    return y

@@ -1,0 +1,154 @@
+from contextlib import ExitStack
+
+import concourse.mybir as mybir
+
+G, D, M, N = 2, 256, 128, 512
+FLOPS = 2 * G * D * M * N
+
+F32 = mybir.dt.float32
+BF16 = mybir.dt.bfloat16
+U32 = mybir.dt.uint32
+U8 = mybir.dt.uint8
+FP8X4 = mybir.dt.float8_e4m3fn_x4
+ALU = mybir.AluOpType
+ACT = mybir.ActivationFunctionType
+
+P = 128
+PACK = 4
+ROWS = D // PACK
+MM_N = 128
+CHUNKS = ((0, 256), (256, 128), (384, 128))
+
+
+def tile_rows_ln_kernel(tc, x, c, gn, gb, out):
+    nc = tc.nc
+    with ExitStack() as ctx:
+        sb = ctx.enter_context(tc.tile_pool(name="sb", bufs=1))
+        ps = ctx.enter_context(tc.psum_pool(name="ps", bufs=1))
+        ctx.enter_context(tc.manual_schedule())
+
+        def operand(name, width):
+            raw = sb.tile([P, PACK, width], F32, name=name + "_raw")
+            packed = sb.tile([P, width, PACK], BF16, name=name + "_bf", align_bytes=64)
+            codes = sb.tile([P, width], U32, name=name + "_codes", align_bytes=64)
+            scales = sb.tile([P, width], U8, name=name + "_scales", align_bytes=64)
+            return raw, packed, codes, scales
+
+        xo = operand("x", M)
+        co = [operand("c%d" % i, w) for i, (n0, w) in enumerate(CHUNKS)]
+        gain = sb.tile([P, G * N], F32, name="gain")
+        bias = sb.tile([P, G * N], F32, name="bias")
+        z = [[ps.tile([M, w], F32, name="z%d_%d" % (g, i)) for i, (n0, w) in enumerate(CHUNKS)] for g in range(G)]
+        stats = [sb.tile([P, 6 * len(CHUNKS)], F32, name="stats%d" % g) for g in range(G)]
+        mv = [sb.tile([P, 2], F32, name="mv%d" % g) for g in range(G)]
+        rstd = [sb.tile([P, 1], F32, name="rstd%d" % g) for g in range(G)]
+        t = [sb.tile([P, N], F32, name="t%d" % g) for g in range(G)]
+        y = [sb.tile([P, N], F32, name="y%d" % g) for g in range(G)]
+        big = sb.tile([P, 1], F32, name="big")
+        eps = sb.tile([P, 1], F32, name="eps")
+
+        xv = x.rearrange("g (p j) m -> (g p) j m", j=PACK)
+        cv = c.rearrange("g (p j) n -> (g p) j n", j=PACK)
+
+        def load_c(i):
+            n0, w = CHUNKS[i]
+            nc.sync.dma_start(out=co[i][0][:], in_=cv[:, :, n0 : n0 + w])
+
+        load_c(0)
+        nc.sync.dma_start(out=xo[0][:], in_=xv)
+        load_c(1)
+        load_c(2)
+        nc.sync.dma_start(out=gain[:], in_=gn.rearrange("g o n -> (g o n)").partition_broadcast(P))
+        nc.sync.dma_start(out=bias[:], in_=gb.rearrange("g o n -> (g o n)").partition_broadcast(P))
+
+        nc.vector.memset(big[:], 1e10)
+        nc.scalar.activation(out=eps[:], in_=big[:], func=ACT.Abs_reciprocal_sqrt)
+
+        def views(op, a, b):
+            src = op[0][:, :, a:b].rearrange("p j (u i) -> p u j i", i=4)
+            dst = op[1][:, a:b, :].rearrange("p (u i) j -> p u j i", i=4)
+            return dst, src
+
+        def cast_v(op, a, b):
+            dst, src = views(op, a, b)
+            nc.vector.tensor_copy(out=dst, in_=src)
+
+        def cast_s(op, a, b):
+            dst, src = views(op, a, b)
+            nc.scalar.copy(out=dst, in_=src)
+
+        def quant(op):
+            nc.vector.quantize_mx(
+                out=op[2][:].bitcast(FP8X4), scales=op[3][:], in_=op[1][:].rearrange("p w j -> p (w j)")
+            )
+
+        def mm(i):
+            w = CHUNKS[i][1]
+            for n0 in range(0, w, MM_N):
+                for g in range(G):
+                    r = slice(g * ROWS, (g + 1) * ROWS)
+                    nc.tensor.matmul_mx(
+                        out=z[g][i][:, n0 : n0 + MM_N],
+                        lhsT=xo[2][r, :].bitcast(FP8X4),
+                        lhsT_scale=xo[3][r, :],
+                        rhs=co[i][2][r, n0 : n0 + MM_N].bitcast(FP8X4),
+                        rhs_scale=co[i][3][r, n0 : n0 + MM_N],
+                        start=True,
+                        stop=True,
+                    )
+
+        def bn(g, i):
+            nc.vector.bn_stats(out=stats[g][:, 6 * i : 6 * i + 6], in_=z[g][i][:])
+
+        def aggr(g):
+            nc.vector.bn_aggr(out=mv[g][:], in_=stats[g][:])
+            nc.scalar.activation(out=rstd[g][:], in_=mv[g][:, 1:2], func=ACT.Abs_reciprocal_sqrt, bias=eps[:])
+
+        def p1(g, i):
+            n0, w = CHUNKS[i]
+            nc.vector.scalar_tensor_tensor(
+                out=t[g][:, n0 : n0 + w], in0=z[g][i][:], scalar=mv[g][:, 0:1],
+                in1=gain[:, g * N + n0 : g * N + n0 + w], op0=ALU.subtract, op1=ALU.mult,
+            )
+
+        def p2(g, a, b, queue):
+            nc.vector.scalar_tensor_tensor(
+                out=y[g][:, a:b], in0=t[g][:, a:b], scalar=rstd[g][:],
+                in1=bias[:, g * N + a : g * N + b], op0=ALU.mult, op1=ALU.add,
+            )
+            queue.dma_start(out=out[g, :, a:b], in_=y[g][:, a:b])
+
+        cast_v(co[0], 0, 160)
+        cast_s(co[0], 160, 256)
+        quant(co[0])
+        cast_s(xo, 64, 128)
+        cast_v(xo, 0, 64)
+        quant(xo)
+        mm(0)
+        cast_s(co[1], 64, 128)
+        cast_v(co[1], 0, 64)
+        quant(co[1])
+        mm(1)
+        bn(0, 0)
+        cast_s(co[2], 64, 128)
+        cast_v(co[2], 0, 64)
+        quant(co[2])
+        mm(2)
+        bn(1, 0)
+        bn(0, 1)
+        bn(0, 2)
+        bn(1, 1)
+        aggr(0)
+        bn(1, 2)
+        p1(0, 0)
+        aggr(1)
+        p1(0, 1)
+        p1(0, 2)
+        p2(0, 0, 256, nc.sync)
+        p1(1, 0)
+        p2(0, 256, 512, nc.scalar)
+        p1(1, 1)
+        p1(1, 2)
+        p2(1, 0, 256, nc.sync)
+        p2(1, 256, 384, nc.scalar)
+        p2(1, 384, 512, nc.sync)

@@ -54,12 +54,16 @@ def tile_rows_ln_kernel(tc, x, c, gn, gb, out):
             n0, w = CHUNKS[i]
             nc.sync.dma_start(out=co[i][0][:], in_=cv[:, :, n0 : n0 + w])
 
+        SEED = 4
+        nc.scalar.dma_start(out=gain[0:P:SEED, :], in_=gn.rearrange("g o n -> (g o n)").partition_broadcast(P // SEED))
+        nc.scalar.dma_start(out=bias[0:P:SEED, :], in_=gb.rearrange("g o n -> (g o n)").partition_broadcast(P // SEED))
         load_c(0)
         nc.sync.dma_start(out=xo[0][:], in_=xv)
         load_c(1)
         load_c(2)
-        nc.sync.dma_start(out=gain[:], in_=gn.rearrange("g o n -> (g o n)").partition_broadcast(P))
-        nc.sync.dma_start(out=bias[:], in_=gb.rearrange("g o n -> (g o n)").partition_broadcast(P))
+        for row in (gain, bias):
+            for r in range(1, SEED):
+                nc.sync.dma_start(out=row[r:P:SEED, :], in_=row[0:P:SEED, :])
 
         nc.vector.memset(big[:], 1e10)
         nc.scalar.activation(out=eps[:], in_=big[:], func=ACT.Abs_reciprocal_sqrt)
@@ -118,30 +122,30 @@ def tile_rows_ln_kernel(tc, x, c, gn, gb, out):
             )
             queue.dma_start(out=out[g, :, a:b], in_=y[g][:, a:b])
 
-        cast_v(co[0], 0, 160)
-        cast_s(co[0], 160, 256)
+        cast_v(co[0], 0, 176)
+        cast_s(co[0], 176, 256)
+        cast_s(xo, 80, 128)
+        cast_v(xo, 0, 80)
         quant(co[0])
-        cast_s(xo, 64, 128)
-        cast_v(xo, 0, 64)
         quant(xo)
         mm(0)
         cast_s(co[1], 64, 128)
         cast_v(co[1], 0, 64)
+        bn(0, 0)
         quant(co[1])
         mm(1)
-        bn(0, 0)
-        cast_s(co[2], 64, 128)
-        cast_v(co[2], 0, 64)
+        cast_s(co[2], 80, 128)
+        cast_v(co[2], 0, 80)
+        bn(1, 0)
         quant(co[2])
         mm(2)
-        bn(1, 0)
         bn(0, 1)
-        bn(0, 2)
         bn(1, 1)
-        aggr(0)
+        bn(0, 2)
         bn(1, 2)
-        p1(0, 0)
+        aggr(0)
         aggr(1)
+        p1(0, 0)
         p1(0, 1)
         p1(0, 2)
         p2(0, 0, 256, nc.sync)

@@ -18,6 +18,7 @@ PACK = 4
 ROWS = D // PACK
 MM_N = 128
 CHUNKS = ((0, 256), (256, 128), (384, 128))
+PARTS = ((0, 384), (384, 128))
 
 
 def tile_rows_ln_kernel(tc, x, c, gn, gb, out):
@@ -36,12 +37,15 @@ def tile_rows_ln_kernel(tc, x, c, gn, gb, out):
 
         xo = operand("x", M)
         co = [operand("c%d" % i, w) for i, (n0, w) in enumerate(CHUNKS)]
-        gain = sb.tile([P, G * N], F32, name="gain")
-        bias = sb.tile([P, G * N], F32, name="bias")
-        z = [[ps.tile([M, w], F32, name="z%d_%d" % (g, i)) for i, (n0, w) in enumerate(CHUNKS)] for g in range(G)]
-        stats = [sb.tile([P, 6 * len(CHUNKS)], F32, name="stats%d" % g) for g in range(G)]
-        mv = [sb.tile([P, 2], F32, name="mv%d" % g) for g in range(G)]
+        gain = [sb.tile([P, N], F32, name="gain%d" % g) for g in range(G)]
+        bias = [sb.tile([P, N], F32, name="bias%d" % g) for g in range(G)]
+        z = [[ps.tile([M, w], F32, name="z%d_%d" % (g, i)) for i, (n0, w) in enumerate(PARTS)] for g in range(G)]
+        part = [[sb.tile([P, 1], F32, name="part%d_%d" % (g, i)) for i in range(len(PARTS))] for g in range(G)]
+        mean = [part[g][-1] for g in range(G)]
+        ssq = [sb.tile([P, 1], F32, name="ssq%d" % g) for g in range(G)]
         rstd = [sb.tile([P, 1], F32, name="rstd%d" % g) for g in range(G)]
+        zs = [sb.tile([P, N], F32, name="zs%d" % g) for g in range(G)]
+        sq = [sb.tile([P, N], F32, name="sq%d" % g) for g in range(G)]
         t = [sb.tile([P, N], F32, name="t%d" % g) for g in range(G)]
         y = [sb.tile([P, N], F32, name="y%d" % g) for g in range(G)]
         big = sb.tile([P, 1], F32, name="big")
@@ -54,19 +58,11 @@ def tile_rows_ln_kernel(tc, x, c, gn, gb, out):
             n0, w = CHUNKS[i]
             nc.sync.dma_start(out=co[i][0][:], in_=cv[:, :, n0 : n0 + w])
 
-        SEED = 4
-        nc.scalar.dma_start(out=gain[0:P:SEED, :], in_=gn.rearrange("g o n -> (g o n)").partition_broadcast(P // SEED))
-        nc.scalar.dma_start(out=bias[0:P:SEED, :], in_=gb.rearrange("g o n -> (g o n)").partition_broadcast(P // SEED))
-        load_c(0)
-        nc.sync.dma_start(out=xo[0][:], in_=xv)
-        load_c(1)
-        load_c(2)
-        for row in (gain, bias):
-            for r in range(1, SEED):
-                nc.sync.dma_start(out=row[r:P:SEED, :], in_=row[0:P:SEED, :])
+        def load_x():
+            nc.sync.dma_start(out=xo[0][:], in_=xv)
 
-        nc.vector.memset(big[:], 1e10)
-        nc.scalar.activation(out=eps[:], in_=big[:], func=ACT.Abs_reciprocal_sqrt)
+        def load_row(dst, src, g):
+            nc.sync.dma_start(out=dst[g][:], in_=src[g, 0, :].partition_broadcast(P))
 
         def views(op, a, b):
             src = op[0][:, :, a:b].rearrange("p j (u i) -> p u j i", i=4)
@@ -87,12 +83,14 @@ def tile_rows_ln_kernel(tc, x, c, gn, gb, out):
             )
 
         def mm(i):
-            w = CHUNKS[i][1]
+            c0, w = CHUNKS[i]
             for n0 in range(0, w, MM_N):
+                k = max(k for k in range(len(PARTS)) if PARTS[k][0] <= c0 + n0)
+                o0 = c0 + n0 - PARTS[k][0]
                 for g in range(G):
                     r = slice(g * ROWS, (g + 1) * ROWS)
                     nc.tensor.matmul_mx(
-                        out=z[g][i][:, n0 : n0 + MM_N],
+                        out=z[g][k][:, o0 : o0 + MM_N],
                         lhsT=xo[2][r, :].bitcast(FP8X4),
                         lhsT_scale=xo[3][r, :],
                         rhs=co[i][2][r, n0 : n0 + MM_N].bitcast(FP8X4),
@@ -101,27 +99,53 @@ def tile_rows_ln_kernel(tc, x, c, gn, gb, out):
                         stop=True,
                     )
 
-        def bn(g, i):
-            nc.vector.bn_stats(out=stats[g][:, 6 * i : 6 * i + 6], in_=z[g][i][:])
+        def sum_s(g, k):
+            n0, w = PARTS[k]
+            nc.scalar.activation(
+                out=zs[g][:, n0 : n0 + w], in_=z[g][k][:], func=ACT.Copy, scale=1.0 / N, accum_out=part[g][k][:]
+            )
 
-        def aggr(g):
-            nc.vector.bn_aggr(out=mv[g][:], in_=stats[g][:])
-            nc.scalar.activation(out=rstd[g][:], in_=mv[g][:, 1:2], func=ACT.Abs_reciprocal_sqrt, bias=eps[:])
+        def sum_v(g, k):
+            n0, w = PARTS[k]
+            nc.vector.tensor_scalar(
+                out=zs[g][:, n0 : n0 + w], in0=z[g][k][:], scalar1=1.0 / N,
+                scalar2=part[g][k - 1][:] if k else None, op0=ALU.mult, op1=ALU.add, accum_out=part[g][k][:],
+            )
 
-        def p1(g, i):
-            n0, w = CHUNKS[i]
+        def var(g):
+            nc.scalar.activation(
+                out=sq[g][:], in_=zs[g][:], func=ACT.Square, scale=-float(N), bias=mean[g][:], accum_out=ssq[g][:]
+            )
+
+        def rs(g):
+            nc.scalar.activation(
+                out=rstd[g][:], in_=ssq[g][:], func=ACT.Abs_reciprocal_sqrt, scale=1.0 / N, bias=eps[:]
+            )
+
+        def p1(g, k):
+            n0, w = PARTS[k]
             nc.vector.scalar_tensor_tensor(
-                out=t[g][:, n0 : n0 + w], in0=z[g][i][:], scalar=mv[g][:, 0:1],
-                in1=gain[:, g * N + n0 : g * N + n0 + w], op0=ALU.subtract, op1=ALU.mult,
+                out=t[g][:, n0 : n0 + w], in0=z[g][k][:], scalar=mean[g][:],
+                in1=gain[g][:, n0 : n0 + w], op0=ALU.subtract, op1=ALU.mult,
             )
 
         def p2(g, a, b, queue):
             nc.vector.scalar_tensor_tensor(
                 out=y[g][:, a:b], in0=t[g][:, a:b], scalar=rstd[g][:],
-                in1=bias[:, g * N + a : g * N + b], op0=ALU.mult, op1=ALU.add,
+                in1=bias[g][:, a:b], op0=ALU.mult, op1=ALU.add,
             )
             queue.dma_start(out=out[g, :, a:b], in_=y[g][:, a:b])
 
+        nc.vector.memset(big[:], 1e10)
+        nc.scalar.activation(out=eps[:], in_=big[:], func=ACT.Abs_reciprocal_sqrt)
+        load_c(0)
+        load_x()
+        load_c(1)
+        load_c(2)
+        load_row(gain, gn, 0)
+        load_row(gain, gn, 1)
+        load_row(bias, gb, 0)
+        load_row(bias, gb, 1)
         cast_v(co[0], 0, 176)
         cast_s(co[0], 176, 256)
         cast_s(xo, 80, 128)
@@ -129,30 +153,28 @@ def tile_rows_ln_kernel(tc, x, c, gn, gb, out):
         quant(co[0])
         quant(xo)
         mm(0)
-        cast_s(co[1], 64, 128)
-        cast_v(co[1], 0, 64)
-        bn(0, 0)
+        cast_s(co[1], 80, 128)
+        cast_v(co[1], 0, 80)
         quant(co[1])
         mm(1)
         cast_s(co[2], 80, 128)
         cast_v(co[2], 0, 80)
-        bn(1, 0)
         quant(co[2])
         mm(2)
-        bn(0, 1)
-        bn(1, 1)
-        bn(0, 2)
-        bn(1, 2)
-        aggr(0)
-        aggr(1)
+        sum_s(0, 0)
+        sum_v(1, 0)
+        sum_v(0, 1)
+        sum_v(1, 1)
+        var(0)
+        rs(0)
+        var(1)
+        rs(1)
         p1(0, 0)
         p1(0, 1)
-        p1(0, 2)
-        p2(0, 0, 256, nc.sync)
         p1(1, 0)
-        p2(0, 256, 512, nc.scalar)
+        p2(0, 0, 256, nc.sync)
         p1(1, 1)
-        p1(1, 2)
+        p2(0, 256, 512, nc.sync)
         p2(1, 0, 256, nc.sync)
-        p2(1, 256, 384, nc.scalar)
+        p2(1, 256, 384, nc.sync)
         p2(1, 384, 512, nc.sync)

@@ -37,8 +37,8 @@ def tile_rows_ln_kernel(tc, x, c, gn, gb, out):
 
         xo = operand("x", M)
         co = [operand("c%d" % i, w) for i, (n0, w) in enumerate(CHUNKS)]
-        gain = [sb.tile([P, N], F32, name="gain%d" % g) for g in range(G)]
-        bias = [sb.tile([P, N], F32, name="bias%d" % g) for g in range(G)]
+        gain = sb.tile([P, G, N], F32, name="gain")
+        bias = sb.tile([P, G, N], F32, name="bias")
         z = [[ps.tile([M, w], F32, name="z%d_%d" % (g, i)) for i, (n0, w) in enumerate(PARTS)] for g in range(G)]
         part = [[sb.tile([P, 1], F32, name="part%d_%d" % (g, i)) for i in range(len(PARTS))] for g in range(G)]
         mean = [part[g][-1] for g in range(G)]
@@ -61,8 +61,11 @@ def tile_rows_ln_kernel(tc, x, c, gn, gb, out):
         def load_x():
             nc.sync.dma_start(out=xo[0][:], in_=xv)
 
-        def load_row(dst, src, g):
-            nc.sync.dma_start(out=dst[g][:], in_=src[g, 0, :].partition_broadcast(P))
+        def load_row(queue, dst, src):
+            queue.dma_start(
+                out=dst[:].rearrange("p g n -> p (g n)"),
+                in_=src.rearrange("g o n -> (g o n)").partition_broadcast(P),
+            )
 
         def views(op, a, b):
             src = op[0][:, :, a:b].rearrange("p j (u i) -> p u j i", i=4)
@@ -126,13 +129,13 @@ def tile_rows_ln_kernel(tc, x, c, gn, gb, out):
             n0, w = PARTS[k]
             nc.vector.scalar_tensor_tensor(
                 out=t[g][:, n0 : n0 + w], in0=z[g][k][:], scalar=mean[g][:],
-                in1=gain[g][:, n0 : n0 + w], op0=ALU.subtract, op1=ALU.mult,
+                in1=gain[:, g, n0 : n0 + w], op0=ALU.subtract, op1=ALU.mult,
             )
 
         def p2(g, a, b, queue):
             nc.vector.scalar_tensor_tensor(
                 out=y[g][:, a:b], in0=t[g][:, a:b], scalar=rstd[g][:],
-                in1=bias[g][:, a:b], op0=ALU.mult, op1=ALU.add,
+                in1=bias[:, g, a:b], op0=ALU.mult, op1=ALU.add,
             )
             queue.dma_start(out=out[g, :, a:b], in_=y[g][:, a:b])
 
@@ -142,12 +145,10 @@ def tile_rows_ln_kernel(tc, x, c, gn, gb, out):
         load_x()
         load_c(1)
         load_c(2)
-        load_row(gain, gn, 0)
-        load_row(gain, gn, 1)
-        load_row(bias, gb, 0)
-        load_row(bias, gb, 1)
+        load_row(nc.sync, bias, gb)
         cast_v(co[0], 0, 176)
         cast_s(co[0], 176, 256)
+        load_row(nc.scalar, gain, gn)
         cast_s(xo, 80, 128)
         cast_v(xo, 0, 80)
         quant(co[0])

@@ -17,8 +17,15 @@ P = 128
 PACK = 4
 ROWS = D // PACK
 MM_N = 128
-CHUNKS = ((0, 256), (256, 128), (384, 128))
-PARTS = ((0, 384), (384, 128))
+BLOCK = 32
+PIECE = 256
+RUN = 4
+INV_EPS_SQUARED = 1e10
+
+LOADS = ((0, 256), (256, 128), (384, 128))
+BANKS = ((0, 384), (384, 128))
+VECTOR_SHARE = (160, 80)
+STORES = ((0, 0, 256), (0, 256, 512), (1, 0, 256), (1, 256, 384), (1, 384, 512))
 
 
 def tile_rows_ln_kernel(tc, x, c, gn, gb, out):
@@ -29,153 +36,177 @@ def tile_rows_ln_kernel(tc, x, c, gn, gb, out):
         ctx.enter_context(tc.manual_schedule())
 
         def operand(name, width):
-            raw = sb.tile([P, PACK, width], F32, name=name + "_raw")
-            packed = sb.tile([P, width, PACK], BF16, name=name + "_bf", align_bytes=64)
-            codes = sb.tile([P, width], U32, name=name + "_codes", align_bytes=64)
-            scales = sb.tile([P, width], U8, name=name + "_scales", align_bytes=64)
-            return raw, packed, codes, scales
+            return {
+                "raw": sb.tile([P, PACK, width], F32, name=name + "_raw"),
+                "bf16": sb.tile([P, width, PACK], BF16, name=name + "_bf16", align_bytes=64),
+                "codes": sb.tile([P, width], U32, name=name + "_codes", align_bytes=64),
+                "scales": sb.tile([P, width], U8, name=name + "_scales", align_bytes=64),
+            }
 
-        xo = operand("x", M)
-        co = [operand("c%d" % i, w) for i, (n0, w) in enumerate(CHUNKS)]
-        gain = sb.tile([P, G, N], F32, name="gain")
+        def per_group(name, width):
+            return [sb.tile([P, width], F32, name="%s%d" % (name, g)) for g in range(G)]
+
+        x_op = operand("x", M)
+        c_ops = [operand("c%d" % i, width) for i, (first, width) in enumerate(LOADS)]
+        gain_rows = sb.tile([P, BLOCK], F32, name="gain_rows", align_bytes=64)
+        gain_cols = sb.tile([P, BLOCK], F32, name="gain_cols", align_bytes=64)
+        gain_wide = sb.tile([P, G * N], F32, name="gain_wide", align_bytes=64)
+        gain = sb.tile([P, G, N], F32, name="gain", align_bytes=64)
         bias = sb.tile([P, G, N], F32, name="bias")
-        z = [[ps.tile([M, w], F32, name="z%d_%d" % (g, i)) for i, (n0, w) in enumerate(PARTS)] for g in range(G)]
-        part = [[sb.tile([P, 1], F32, name="part%d_%d" % (g, i)) for i in range(len(PARTS))] for g in range(G)]
-        mean = [part[g][-1] for g in range(G)]
-        ssq = [sb.tile([P, 1], F32, name="ssq%d" % g) for g in range(G)]
-        rstd = [sb.tile([P, 1], F32, name="rstd%d" % g) for g in range(G)]
-        zs = [sb.tile([P, N], F32, name="zs%d" % g) for g in range(G)]
-        sq = [sb.tile([P, N], F32, name="sq%d" % g) for g in range(G)]
-        t = [sb.tile([P, N], F32, name="t%d" % g) for g in range(G)]
-        y = [sb.tile([P, N], F32, name="y%d" % g) for g in range(G)]
-        big = sb.tile([P, 1], F32, name="big")
+        z = [[ps.tile([M, width], F32, name="z%d_%d" % (g, k)) for k, (first, width) in enumerate(BANKS)] for g in range(G)]
+        head_mean = per_group("head_mean", 1)
+        mean = per_group("mean", 1)
+        sum_sq = per_group("sum_sq", 1)
+        rstd = per_group("rstd", 1)
+        z_scaled = per_group("z_scaled", N)
+        squares = per_group("squares", N)
+        gained = per_group("gained", N)
+        result = per_group("result", N)
+        inv_eps_squared = sb.tile([P, 1], F32, name="inv_eps_squared")
         eps = sb.tile([P, 1], F32, name="eps")
 
-        xv = x.rearrange("g (p j) m -> (g p) j m", j=PACK)
-        cv = c.rearrange("g (p j) n -> (g p) j n", j=PACK)
-
         def load_c(i):
-            n0, w = CHUNKS[i]
-            nc.sync.dma_start(out=co[i][0][:], in_=cv[:, :, n0 : n0 + w])
+            first, width = LOADS[i]
+            rows = c.rearrange("g (p j) n -> (g p) j n", j=PACK)
+            nc.sync.dma_start(out=c_ops[i]["raw"][:], in_=rows[:, :, first : first + width])
 
-        def load_x():
-            nc.sync.dma_start(out=xo[0][:], in_=xv)
-
-        def load_row(queue, dst, src):
-            queue.dma_start(
+        def load_on_all_partitions(dst, src):
+            nc.sync.dma_start(
                 out=dst[:].rearrange("p g n -> p (g n)"),
                 in_=src.rearrange("g o n -> (g o n)").partition_broadcast(P),
             )
 
-        def views(op, a, b):
-            src = op[0][:, :, a:b].rearrange("p j (u i) -> p u j i", i=4)
-            dst = op[1][:, a:b, :].rearrange("p (u i) j -> p u j i", i=4)
-            return dst, src
-
-        def cast_v(op, a, b):
-            dst, src = views(op, a, b)
-            nc.vector.tensor_copy(out=dst, in_=src)
-
-        def cast_s(op, a, b):
-            dst, src = views(op, a, b)
-            nc.scalar.copy(out=dst, in_=src)
-
-        def quant(op):
-            nc.vector.quantize_mx(
-                out=op[2][:].bitcast(FP8X4), scales=op[3][:], in_=op[1][:].rearrange("p w j -> p (w j)")
+        def widen_gain(copy, first, end):
+            blocks = slice(first // BLOCK, end // BLOCK)
+            copy(
+                out=gain_wide[:, first:end].rearrange("p (b i) -> p b i", i=BLOCK),
+                in_=gain_cols[:, blocks].unsqueeze(2).to_broadcast([P, (end - first) // BLOCK, BLOCK]),
             )
 
-        def mm(i):
-            c0, w = CHUNKS[i]
-            for n0 in range(0, w, MM_N):
-                k = max(k for k in range(len(PARTS)) if PARTS[k][0] <= c0 + n0)
-                o0 = c0 + n0 - PARTS[k][0]
+        def turn_gain(piece):
+            cols = slice(piece * PIECE, (piece + 1) * PIECE)
+            nc.vector.transpose(out=gain[:].rearrange("p g n -> p (g n)")[:, cols], in_=gain_wide[:, cols])
+
+        def interleave(copy, op, first, end):
+            copy(
+                out=op["bf16"][:, first:end, :].rearrange("p (u i) j -> p u j i", i=RUN),
+                in_=op["raw"][:, :, first:end].rearrange("p j (u i) -> p u j i", i=RUN),
+            )
+
+        def cast(op, split):
+            interleave(nc.vector.tensor_copy, op, 0, split)
+            interleave(nc.scalar.copy, op, split, op["raw"].shape[2])
+
+        def quantize(op):
+            nc.vector.quantize_mx(
+                out=op["codes"][:].bitcast(FP8X4),
+                scales=op["scales"][:],
+                in_=op["bf16"][:].rearrange("p w j -> p (w j)"),
+            )
+
+        def multiply(i):
+            first, width = LOADS[i]
+            for col in range(0, width, MM_N):
+                k = 0 if first + col < BANKS[1][0] else 1
+                place = first + col - BANKS[k][0]
                 for g in range(G):
-                    r = slice(g * ROWS, (g + 1) * ROWS)
+                    rows = slice(g * ROWS, (g + 1) * ROWS)
                     nc.tensor.matmul_mx(
-                        out=z[g][k][:, o0 : o0 + MM_N],
-                        lhsT=xo[2][r, :].bitcast(FP8X4),
-                        lhsT_scale=xo[3][r, :],
-                        rhs=co[i][2][r, n0 : n0 + MM_N].bitcast(FP8X4),
-                        rhs_scale=co[i][3][r, n0 : n0 + MM_N],
+                        out=z[g][k][:, place : place + MM_N],
+                        lhsT=x_op["codes"][rows, :].bitcast(FP8X4),
+                        lhsT_scale=x_op["scales"][rows, :],
+                        rhs=c_ops[i]["codes"][rows, col : col + MM_N].bitcast(FP8X4),
+                        rhs_scale=c_ops[i]["scales"][rows, col : col + MM_N],
                         start=True,
                         stop=True,
                     )
 
-        def sum_s(g, k):
-            n0, w = PARTS[k]
-            nc.scalar.activation(
-                out=zs[g][:, n0 : n0 + w], in_=z[g][k][:], func=ACT.Copy, scale=1.0 / N, accum_out=part[g][k][:]
-            )
+        def bank_columns(k):
+            first, width = BANKS[k]
+            return slice(first, first + width)
 
-        def sum_v(g, k):
-            n0, w = PARTS[k]
+        def vector_sum(g, k, start_from, total):
             nc.vector.tensor_scalar(
-                out=zs[g][:, n0 : n0 + w], in0=z[g][k][:], scalar1=1.0 / N,
-                scalar2=part[g][k - 1][:] if k else None, op0=ALU.mult, op1=ALU.add, accum_out=part[g][k][:],
+                out=z_scaled[g][:, bank_columns(k)],
+                in0=z[g][k][:],
+                scalar1=1.0 / N,
+                scalar2=start_from,
+                op0=ALU.mult,
+                op1=ALU.add,
+                accum_out=total,
             )
 
-        def var(g):
-            nc.scalar.activation(
-                out=sq[g][:], in_=zs[g][:], func=ACT.Square, scale=-float(N), bias=mean[g][:], accum_out=ssq[g][:]
-            )
+        for q, queue in enumerate((nc.sync, nc.scalar, nc.sync, nc.scalar)):
+            queue.dma_start(out=gain_rows[q * BLOCK : (q + 1) * BLOCK, :], in_=gn.rearrange("g o (b j) -> (g o b) j", j=BLOCK))
 
-        def rs(g):
-            nc.scalar.activation(
-                out=rstd[g][:], in_=ssq[g][:], func=ACT.Abs_reciprocal_sqrt, scale=1.0 / N, bias=eps[:]
-            )
+        nc.vector.memset(inv_eps_squared[:], INV_EPS_SQUARED)
+        nc.scalar.activation(out=eps[:], in_=inv_eps_squared[:], func=ACT.Abs_reciprocal_sqrt)
 
-        def p1(g, k):
-            n0, w = PARTS[k]
-            nc.vector.scalar_tensor_tensor(
-                out=t[g][:, n0 : n0 + w], in0=z[g][k][:], scalar=mean[g][:],
-                in1=gain[:, g, n0 : n0 + w], op0=ALU.subtract, op1=ALU.mult,
-            )
-
-        def p2(g, a, b, queue):
-            nc.vector.scalar_tensor_tensor(
-                out=y[g][:, a:b], in0=t[g][:, a:b], scalar=rstd[g][:],
-                in1=bias[:, g, a:b], op0=ALU.mult, op1=ALU.add,
-            )
-            queue.dma_start(out=out[g, :, a:b], in_=y[g][:, a:b])
-
-        nc.vector.memset(big[:], 1e10)
-        nc.scalar.activation(out=eps[:], in_=big[:], func=ACT.Abs_reciprocal_sqrt)
         load_c(0)
-        load_x()
+        nc.sync.dma_start(out=x_op["raw"][:], in_=x.rearrange("g (p j) m -> (g p) j m", j=PACK))
         load_c(1)
         load_c(2)
-        load_row(nc.sync, bias, gb)
-        cast_v(co[0], 0, 176)
-        cast_s(co[0], 176, 256)
-        load_row(nc.scalar, gain, gn)
-        cast_s(xo, 80, 128)
-        cast_v(xo, 0, 80)
-        quant(co[0])
-        quant(xo)
-        mm(0)
-        cast_s(co[1], 80, 128)
-        cast_v(co[1], 0, 80)
-        quant(co[1])
-        mm(1)
-        cast_s(co[2], 80, 128)
-        cast_v(co[2], 0, 80)
-        quant(co[2])
-        mm(2)
-        sum_s(0, 0)
-        sum_v(1, 0)
-        sum_v(0, 1)
-        sum_v(1, 1)
-        var(0)
-        rs(0)
-        var(1)
-        rs(1)
-        p1(0, 0)
-        p1(0, 1)
-        p1(1, 0)
-        p2(0, 0, 256, nc.sync)
-        p1(1, 1)
-        p2(0, 256, 512, nc.sync)
-        p2(1, 0, 256, nc.sync)
-        p2(1, 256, 384, nc.sync)
-        p2(1, 384, 512, nc.sync)
+        load_on_all_partitions(bias, gb)
+
+        nc.vector.transpose(out=gain_cols[:], in_=gain_rows[:])
+        widen_gain(nc.vector.tensor_copy, 0, PIECE)
+        widen_gain(nc.vector.tensor_copy, PIECE, N)
+        widen_gain(nc.scalar.copy, N, G * N)
+        turn_gain(0)
+
+        cast(c_ops[0], VECTOR_SHARE[0])
+        interleave(nc.scalar.copy, x_op, 0, M)
+        interleave(nc.scalar.copy, c_ops[1], 0, LOADS[1][1])
+        turn_gain(1)
+        quantize(c_ops[0])
+        turn_gain(2)
+        quantize(x_op)
+        multiply(0)
+        quantize(c_ops[1])
+        multiply(1)
+        cast(c_ops[2], VECTOR_SHARE[1])
+        turn_gain(3)
+        quantize(c_ops[2])
+        multiply(2)
+
+        nc.scalar.activation(
+            out=z_scaled[0][:, bank_columns(0)], in_=z[0][0][:], func=ACT.Copy, scale=1.0 / N, accum_out=head_mean[0][:]
+        )
+        vector_sum(1, 0, None, head_mean[1][:])
+        for g in range(G):
+            vector_sum(g, 1, head_mean[g][:], mean[g][:])
+
+        for g in range(G):
+            nc.scalar.activation(
+                out=squares[g][:],
+                in_=z_scaled[g][:],
+                func=ACT.Square,
+                scale=-float(N),
+                bias=mean[g][:],
+                accum_out=sum_sq[g][:],
+            )
+            nc.scalar.activation(
+                out=rstd[g][:], in_=sum_sq[g][:], func=ACT.Abs_reciprocal_sqrt, scale=1.0 / N, bias=eps[:]
+            )
+
+        for g in range(G):
+            for k in range(len(BANKS)):
+                nc.vector.scalar_tensor_tensor(
+                    out=gained[g][:, bank_columns(k)],
+                    in0=z[g][k][:],
+                    scalar=mean[g][:],
+                    in1=gain[:, g, bank_columns(k)],
+                    op0=ALU.subtract,
+                    op1=ALU.mult,
+                )
+
+        for g, first, end in STORES:
+            nc.vector.scalar_tensor_tensor(
+                out=result[g][:, first:end],
+                in0=gained[g][:, first:end],
+                scalar=rstd[g][:],
+                in1=bias[:, g, first:end],
+                op0=ALU.mult,
+                op1=ALU.add,
+            )
+            nc.sync.dma_start(out=out[g, :, first:end], in_=result[g][:, first:end])

from contextlib import ExitStack

import concourse.mybir as mybir

G, D, M, N = 2, 256, 128, 512
FLOPS = 2 * G * D * M * N

F32 = mybir.dt.float32
BF16 = mybir.dt.bfloat16
U32 = mybir.dt.uint32
U8 = mybir.dt.uint8
FP8X4 = mybir.dt.float8_e4m3fn_x4
ALU = mybir.AluOpType
ACT = mybir.ActivationFunctionType

P = 128
PACK = 4
ROWS = D // PACK
MM_N = 128
BLOCK = 32
PIECE = 256
RUN = 4
INV_EPS_SQUARED = 1e10

LOADS = ((0, 256), (256, 128), (384, 128))
BANKS = ((0, 384), (384, 128))
VECTOR_SHARE = (160, 80)
STORES = ((0, 0, 256), (0, 256, 512), (1, 0, 256), (1, 256, 384), (1, 384, 512))


def tile_rows_ln_kernel(tc, x, c, gn, gb, out):
    nc = tc.nc
    with ExitStack() as ctx:
        sb = ctx.enter_context(tc.tile_pool(name="sb", bufs=1))
        ps = ctx.enter_context(tc.psum_pool(name="ps", bufs=1))
        ctx.enter_context(tc.manual_schedule())

        def operand(name, width):
            return {
                "raw": sb.tile([P, PACK, width], F32, name=name + "_raw"),
                "bf16": sb.tile([P, width, PACK], BF16, name=name + "_bf16", align_bytes=64),
                "codes": sb.tile([P, width], U32, name=name + "_codes", align_bytes=64),
                "scales": sb.tile([P, width], U8, name=name + "_scales", align_bytes=64),
            }

        def per_group(name, width):
            return [sb.tile([P, width], F32, name="%s%d" % (name, g)) for g in range(G)]

        x_op = operand("x", M)
        c_ops = [operand("c%d" % i, width) for i, (first, width) in enumerate(LOADS)]
        gain_rows = sb.tile([P, BLOCK], F32, name="gain_rows", align_bytes=64)
        gain_cols = sb.tile([P, BLOCK], F32, name="gain_cols", align_bytes=64)
        gain_wide = sb.tile([P, G * N], F32, name="gain_wide", align_bytes=64)
        gain = sb.tile([P, G, N], F32, name="gain", align_bytes=64)
        bias = sb.tile([P, G, N], F32, name="bias")
        z = [[ps.tile([M, width], F32, name="z%d_%d" % (g, k)) for k, (first, width) in enumerate(BANKS)] for g in range(G)]
        head_mean = per_group("head_mean", 1)
        mean = per_group("mean", 1)
        sum_sq = per_group("sum_sq", 1)
        rstd = per_group("rstd", 1)
        z_scaled = per_group("z_scaled", N)
        squares = per_group("squares", N)
        gained = per_group("gained", N)
        result = per_group("result", N)
        inv_eps_squared = sb.tile([P, 1], F32, name="inv_eps_squared")
        eps = sb.tile([P, 1], F32, name="eps")

        def load_c(i):
            first, width = LOADS[i]
            rows = c.rearrange("g (p j) n -> (g p) j n", j=PACK)
            nc.sync.dma_start(out=c_ops[i]["raw"][:], in_=rows[:, :, first : first + width])

        def load_on_all_partitions(dst, src):
            nc.sync.dma_start(
                out=dst[:].rearrange("p g n -> p (g n)"),
                in_=src.rearrange("g o n -> (g o n)").partition_broadcast(P),
            )

        def widen_gain(copy, first, end):
            blocks = slice(first // BLOCK, end // BLOCK)
            copy(
                out=gain_wide[:, first:end].rearrange("p (b i) -> p b i", i=BLOCK),
                in_=gain_cols[:, blocks].unsqueeze(2).to_broadcast([P, (end - first) // BLOCK, BLOCK]),
            )

        def turn_gain(piece):
            cols = slice(piece * PIECE, (piece + 1) * PIECE)
            nc.vector.transpose(out=gain[:].rearrange("p g n -> p (g n)")[:, cols], in_=gain_wide[:, cols])

        def interleave(copy, op, first, end):
            copy(
                out=op["bf16"][:, first:end, :].rearrange("p (u i) j -> p u j i", i=RUN),
                in_=op["raw"][:, :, first:end].rearrange("p j (u i) -> p u j i", i=RUN),
            )

        def cast(op, split):
            interleave(nc.vector.tensor_copy, op, 0, split)
            interleave(nc.scalar.copy, op, split, op["raw"].shape[2])

        def quantize(op):
            nc.vector.quantize_mx(
                out=op["codes"][:].bitcast(FP8X4),
                scales=op["scales"][:],
                in_=op["bf16"][:].rearrange("p w j -> p (w j)"),
            )

        def multiply(i):
            first, width = LOADS[i]
            for col in range(0, width, MM_N):
                k = 0 if first + col < BANKS[1][0] else 1
                place = first + col - BANKS[k][0]
                for g in range(G):
                    rows = slice(g * ROWS, (g + 1) * ROWS)
                    nc.tensor.matmul_mx(
                        out=z[g][k][:, place : place + MM_N],
                        lhsT=x_op["codes"][rows, :].bitcast(FP8X4),
                        lhsT_scale=x_op["scales"][rows, :],
                        rhs=c_ops[i]["codes"][rows, col : col + MM_N].bitcast(FP8X4),
                        rhs_scale=c_ops[i]["scales"][rows, col : col + MM_N],
                        start=True,
                        stop=True,
                    )

        def bank_columns(k):
            first, width = BANKS[k]
            return slice(first, first + width)

        def vector_sum(g, k, start_from, total):
            nc.vector.tensor_scalar(
                out=z_scaled[g][:, bank_columns(k)],
                in0=z[g][k][:],
                scalar1=1.0 / N,
                scalar2=start_from,
                op0=ALU.mult,
                op1=ALU.add,
                accum_out=total,
            )

        for q, queue in enumerate((nc.sync, nc.scalar, nc.sync, nc.scalar)):
            queue.dma_start(out=gain_rows[q * BLOCK : (q + 1) * BLOCK, :], in_=gn.rearrange("g o (b j) -> (g o b) j", j=BLOCK))

        nc.vector.memset(inv_eps_squared[:], INV_EPS_SQUARED)
        nc.scalar.activation(out=eps[:], in_=inv_eps_squared[:], func=ACT.Abs_reciprocal_sqrt)

        load_c(0)
        nc.sync.dma_start(out=x_op["raw"][:], in_=x.rearrange("g (p j) m -> (g p) j m", j=PACK))
        load_c(1)
        load_c(2)
        load_on_all_partitions(bias, gb)

        nc.vector.transpose(out=gain_cols[:], in_=gain_rows[:])
        widen_gain(nc.vector.tensor_copy, 0, PIECE)
        widen_gain(nc.vector.tensor_copy, PIECE, N)
        widen_gain(nc.scalar.copy, N, G * N)
        turn_gain(0)

        cast(c_ops[0], VECTOR_SHARE[0])
        interleave(nc.scalar.copy, x_op, 0, M)
        interleave(nc.scalar.copy, c_ops[1], 0, LOADS[1][1])
        turn_gain(1)
        quantize(c_ops[0])
        turn_gain(2)
        quantize(x_op)
        multiply(0)
        quantize(c_ops[1])
        multiply(1)
        cast(c_ops[2], VECTOR_SHARE[1])
        turn_gain(3)
        quantize(c_ops[2])
        multiply(2)

        nc.scalar.activation(
            out=z_scaled[0][:, bank_columns(0)], in_=z[0][0][:], func=ACT.Copy, scale=1.0 / N, accum_out=head_mean[0][:]
        )
        vector_sum(1, 0, None, head_mean[1][:])
        for g in range(G):
            vector_sum(g, 1, head_mean[g][:], mean[g][:])

        for g in range(G):
            nc.scalar.activation(
                out=squares[g][:],
                in_=z_scaled[g][:],
                func=ACT.Square,
                scale=-float(N),
                bias=mean[g][:],
                accum_out=sum_sq[g][:],
            )
            nc.scalar.activation(
                out=rstd[g][:], in_=sum_sq[g][:], func=ACT.Abs_reciprocal_sqrt, scale=1.0 / N, bias=eps[:]
            )

        for g in range(G):
            for k in range(len(BANKS)):
                nc.vector.scalar_tensor_tensor(
                    out=gained[g][:, bank_columns(k)],
                    in0=z[g][k][:],
                    scalar=mean[g][:],
                    in1=gain[:, g, bank_columns(k)],
                    op0=ALU.subtract,
                    op1=ALU.mult,
                )

        for g, first, end in STORES:
            nc.vector.scalar_tensor_tensor(
                out=result[g][:, first:end],
                in0=gained[g][:, first:end],
                scalar=rstd[g][:],
                in1=bias[:, g, first:end],
                op0=ALU.mult,
                op1=ALU.add,
            )
            nc.sync.dma_start(out=out[g, :, first:end], in_=result[g][:, first:end])
